import numpy as np, ml_dtypes
CORES = [2,34,66,98,130,162,194,226,258,290,322,354,386,418,450,482]
N = 16
TK = 64
def setup_inputs(rng):
    rt = (0.75 * rng.standard_normal((128, 1), dtype=np.float32) + rng.standard_normal((128, N), dtype=np.float32) / 2).astype(ml_dtypes.bfloat16)
    return {"x": rng.standard_normal((N, 128, TK), dtype=np.float32).astype(ml_dtypes.bfloat16), "rt": np.broadcast_to(rt, (N, 128, N)).copy(), "w": rng.standard_normal((N, 128, 128), dtype=np.float32).astype(ml_dtypes.bfloat16)}
def setup_inputs_big(rng):
    d = setup_inputs(rng)
    for k in ("x", "w"): d[k] = (d[k].astype(np.float32) * 1024.0).astype(d[k].dtype)
    return d
def setup_inputs_small(rng):
    d = setup_inputs(rng)
    for k in ("x", "w"): d[k] = (d[k].astype(np.float32) * (1 / 1024.0)).astype(d[k].dtype)
    return d
def reference(x, rt, w):
    X, RT, W = x.astype(np.float64), rt.astype(np.float64), w.astype(np.float64)
    y = np.zeros((N, 128, TK))
    for r in range(N):
        sc = RT[r].T @ X[r]
        g = np.exp(sc - sc.max(axis=0)); g = g / g.sum(axis=0)
        y[r] = sum(g[j] * (W[j].T @ X[r]) for j in range(N))
    return {"y": y.astype(ml_dtypes.bfloat16)}

@@ -1,0 +1,151 @@
+from concourse.bass import DstId, RemoteDMATransfer
+from concourse.mybir import AluOpType, AxisListType, ActivationFunctionType
+
+NG = 8
+TK = 64
+DM = 128
+
+SCRATCH = {
+    "xs": ("sbuf", [128, 2 * TK], "bfloat16"),
+    "rts": ("sbuf", [128, 16], "bfloat16"),
+    "wall": ("sbuf", [128, NG * DM], "bfloat16"),
+    "ident": ("sbuf", [128, 128], "bfloat16"),
+    "sm_o": ("sbuf", [128, 4], "float32"),
+    "sm_p": ("sbuf", [128, 4], "float32"),
+    "ex_o": ("sbuf", [128, 16], "float32"),
+    "ex_p": ("sbuf", [128, 16], "float32"),
+    "xts_o": ("sbuf", [128, 128], "bfloat16"),
+    "xts_p": ("sbuf", [128, 128], "bfloat16"),
+    "dg_o": ("sbuf", [128, NG * TK], "bfloat16"),
+    "dg_p": ("sbuf", [128, NG * TK], "bfloat16"),
+    "xg_o": ("sbuf", [128, NG * TK], "bfloat16"),
+    "xg_p": ("sbuf", [128, NG * TK], "bfloat16"),
+    "yp": ("sbuf", [128, TK], "bfloat16"),
+    "yr": ("sbuf", [128, TK], "bfloat16"),
+    "ysb": ("sbuf", [128, TK], "bfloat16"),
+    "st": ("psum", [128, 512], "float32"),
+    "xt": ("psum", [128, 1024], "bfloat16"),
+    "pga": ("psum", [128, 512], "float32"),
+    "pgb": ("psum", [128, 512], "float32"),
+    "acc_p": ("psum", [128, 512], "float32"),
+    "acc_o": ("psum", [128, 512], "float32"),
+}
+_STAGES = ["st", "xt", "nm", "ex", "xts", "ri", "da", "db", "pa", "pb", "ca", "cb"]
+SEMAPHORES = (["ldx", "ldw", "ldrt", "ones", "idn", "xarr", "sent", "accp", "acco", "ypr", "yarr", "ysum", "stored"]
+              + ["w%d" % i for i in range(NG)]
+              + [s + "_" + h for h in ("o", "p") for s in _STAGES])
+
+
+def _engines(mask):
+    return bin(mask).count("1")
+
+
+def rank_program(g, core, T, topo):
+    if T.rank_of(core) is None:
+        return
+    S = T.sem
+    cores = list(T.cores)
+    group = [q for q in cores if q == core or topo.same_plane(core, q)]
+    me = group.index(core)
+    partner = [q for q in cores if topo.rack(topo.host(q)) != topo.rack(topo.host(core))
+               and topo.may_write(core, q) and topo.chip(q) == topo.chip(core)][0]
+    peers = [group[(me + k) % NG] for k in range(1, NG)]
+    H = NG // 2
+
+    def slot(i):
+        return T.wall[:, i * DM:(i + 1) * DM]
+
+    g.sync.dma_start(T.xs[:, 0:TK], T.x[:]).then_inc(S.ldx, 16)
+    g.scalar.dma_start(slot(me), T.w[:]).then_inc(S.ldw, 16)
+    g.sync.dma_start(T.rts[:], T.rt[:]).then_inc(S.ldrt, 16)
+
+    g.vector.memset(T.ident[:], 1.0).then_inc(S.ones, 1)
+    g.wait_ge(S.ones, 1)
+    g.affine_select(T.ident[:], T.ident[:], [[-1, 128]], AluOpType.is_equal, 0.0, 0, 1).then_inc(S.idn, 1)
+
+    prid, ppid = topo.addr(partner, core)
+    pmask = topo.mask(core, partner)
+    g.wait_ge(S.ldx, 16)
+    g.remote_dma(out_ap=T.xs[:, TK:2 * TK], in_ap=T.xs[:, 0:TK], remote_sem=S.xarr, local_sem=S.sent,
+                 pid=ppid, routing_id=prid, dma_engine_mask=pmask)
+
+    wmask = pmask
+    for q in peers:
+        wmask &= topo.mask(core, q)
+    ids = []
+    for q in peers:
+        rid, pid = topo.addr(q, core)
+        ids.append(DstId(rid=rid, pnc=pid))
+    g.wait_ge(S.ldw, 16)
+    g.remote_dma_fused([RemoteDMATransfer(dst_ids=ids, dma_engine_mask=wmask, remote_sem=S["w%d" % me],
+                                          srcs=[slot(me)], dsts=[slot(me) for _ in peers], alu_op=0)],
+                       local_sem=S.sent)
+
+    def half(h, xh, first):
+        sm, ex, xts, dg, xg = T["sm_" + h], T["ex_" + h], T["xts_" + h], T["dg_" + h], T["xg_" + h]
+        s = {n: S[n + "_" + h] for n in _STAGES}
+        nm, su, ri = sm[0:TK, 0:1], sm[0:TK, 1:2], sm[0:TK, 2:3]
+        g.tensor.matmul(T.st[0:TK, 0:16], xh, T.rts[:], True, True).then_inc(s["st"], 1)
+        g.tensor.transpose(T.xt[0:TK, 0:128], xh, T.ident[:]).then_inc(s["xt"], 1)
+        g.vector.wait_ge(s["st"], 1)
+        g.vector.tensor_reduce(nm, T.st[0:TK, 0:16], AxisListType.X, AluOpType.max, negate=True).then_inc(s["nm"], 1)
+        g.scalar.wait_ge(s["nm"], 1)
+        g.scalar.activation(ex[0:TK, :], T.st[0:TK, 0:16], ActivationFunctionType.Exp, bias=nm, scale=1.0,
+                            accum_out=su).then_inc(s["ex"], 1)
+        g.vector.wait_ge(s["xt"], 1)
+        g.vector.tensor_copy(xts[0:TK, :], T.xt[0:TK, 0:128]).then_inc(s["xts"], 1)
+        g.vector.wait_ge(s["ex"], 1)
+        g.vector.reciprocal(ri, su).then_inc(s["ri"], 1)
+        g.vector.wait_ge(s["ri"], 1)
+        for i, q in enumerate(group):
+            j = T.rank_of(q)
+            g.vector.tensor_scalar(dg[0:TK, i * TK:(i + 1) * TK], T.ident[0:TK, 0:TK], ex[0:TK, j:j + 1], ri,
+                                   AluOpType.mult, AluOpType.mult).then_inc(s["da"] if i < H else s["db"], 1)
+        g.tensor.wait_ge(s["xts"], 1)
+        if not first:
+            g.tensor.wait_ge(S.ca_o, 1)
+            g.tensor.wait_ge(S.cb_o, 1)
+        g.tensor.wait_ge(s["da"], H)
+        g.tensor.matmul(T.pga[:, 0:H * TK], xts[0:TK, :], dg[0:TK, 0:H * TK], True, True).then_inc(s["pa"], 1)
+        g.tensor.wait_ge(s["db"], NG - H)
+        g.tensor.matmul(T.pgb[:, 0:H * TK], xts[0:TK, :], dg[0:TK, H * TK:NG * TK], True, True).then_inc(s["pb"], 1)
+        g.vector.wait_ge(s["pa"], 1)
+        g.vector.tensor_copy(xg[:, 0:H * TK], T.pga[:, 0:H * TK]).then_inc(s["ca"], 1)
+        g.scalar.wait_ge(s["pb"], 1)
+        g.scalar.activation(xg[:, H * TK:NG * TK], T.pgb[:, 0:H * TK], ActivationFunctionType.Copy).then_inc(s["cb"], 1)
+
+    g.tensor.wait_ge(S.ldx, 16)
+    g.tensor.wait_ge(S.ldrt, 16)
+    g.tensor.wait_ge(S.idn, 1)
+    g.vector.wait_ge(S.idn, 1)
+    half("o", T.xs[:, 0:TK], True)
+    g.tensor.wait_ge(S.xarr, _engines(pmask))
+    half("p", T.xs[:, TK:2 * TK], False)
+
+    g.tensor.wait_ge(S.ca_p, 1)
+    g.tensor.wait_ge(S.cb_p, 1)
+    order = [me] + [(me - k) % NG for k in range(1, NG)]
+    for n, i in enumerate(order):
+        if i == me:
+            g.tensor.wait_ge(S.ldw, 16)
+        else:
+            g.tensor.wait_ge(S["w%d" % i], _engines(wmask))
+        a = g.tensor.matmul(T.acc_p[:, 0:TK], slot(i), T.xg_p[:, i * TK:(i + 1) * TK], n == 0, n == NG - 1)
+        b = g.tensor.matmul(T.acc_o[:, 0:TK], slot(i), T.xg_o[:, i * TK:(i + 1) * TK], n == 0, n == NG - 1)
+        if n == NG - 1:
+            a.then_inc(S.accp, 1)
+            b.then_inc(S.acco, 1)
+
+    g.vector.wait_ge(S.accp, 1)
+    g.vector.tensor_copy(T.yp[:], T.acc_p[:, 0:TK]).then_inc(S.ypr, 1)
+    g.wait_ge(S.ypr, 1)
+    g.remote_dma(out_ap=T.yr[:], in_ap=T.yp[:], remote_sem=S.yarr, local_sem=S.sent,
+                 pid=ppid, routing_id=prid, dma_engine_mask=pmask)
+
+    g.vector.wait_ge(S.acco, 1)
+    g.vector.wait_ge(S.yarr, _engines(pmask))
+    g.vector.tensor_tensor(T.ysb[:], T.acc_o[:, 0:TK], T.yr[:], AluOpType.add).then_inc(S.ysum, 1)
+    g.sync.wait_ge(S.ysum, 1)
+    g.sync.dma_start(T.y[:], T.ysb[:]).then_inc(S.stored, 16)
+    g.sync.wait_ge(S.stored, 16)
+    g.wait_ge(S.sent, 2 * _engines(pmask) + _engines(wmask))

@@ -4,6 +4,9 @@ from concourse.mybir import AluOpType, AxisListType, ActivationFunctionType
 NG = 8
 TK = 64
 DM = 128
+NP = 4
+EP = NG // NP
+NS = 6
 
 SCRATCH = {
     "xs": ("sbuf", [128, 2 * TK], "bfloat16"),
@@ -25,12 +28,15 @@ SCRATCH = {
     "ysb": ("sbuf", [128, TK], "bfloat16"),
     "st": ("psum", [128, 512], "float32"),
     "xt": ("psum", [128, 1024], "bfloat16"),
-    "pga": ("psum", [128, 512], "float32"),
-    "pgb": ("psum", [128, 512], "float32"),
+    "pg0": ("psum", [128, 512], "float32"),
+    "pg1": ("psum", [128, 512], "float32"),
+    "pg2": ("psum", [128, 512], "float32"),
+    "pg3": ("psum", [128, 512], "float32"),
     "acc_p": ("psum", [128, 512], "float32"),
     "acc_o": ("psum", [128, 512], "float32"),
 }
-_STAGES = ["st", "xt", "nm", "ex", "xts", "ri", "da", "db", "pa", "pb", "ca", "cb"]
+_STAGES = (["st", "xt", "nm", "ex", "ri", "xts"] + ["d%d" % q for q in range(NP)] + ["p%d" % q for q in range(NP)]
+           + ["c%d" % q for q in range(NP)])
 SEMAPHORES = (["ldx", "ldw", "ldrt", "ones", "idn", "xarr", "sent", "accp", "acco", "ypr", "yarr", "ysum", "stored"]
               + ["w%d" % i for i in range(NG)]
               + [s + "_" + h for h in ("o", "p") for s in _STAGES])
@@ -50,7 +56,7 @@ def rank_program(g, core, T, topo):
     partner = [q for q in cores if topo.rack(topo.host(q)) != topo.rack(topo.host(core))
                and topo.may_write(core, q) and topo.chip(q) == topo.chip(core)][0]
     peers = [group[(me + k) % NG] for k in range(1, NG)]
-    H = NG // 2
+    order = [me] + [(me - k) % NG for k in range(1, NG)]
 
     def slot(i):
         return T.wall[:, i * DM:(i + 1) * DM]
@@ -85,6 +91,12 @@ def rank_program(g, core, T, topo):
         sm, ex, xts, dg, xg = T["sm_" + h], T["ex_" + h], T["xts_" + h], T["dg_" + h], T["xg_" + h]
         s = {n: S[n + "_" + h] for n in _STAGES}
         nm, su, ri = sm[0:TK, 0:1], sm[0:TK, 1:2], sm[0:TK, 2:3]
+        eye = T.ident[0:TK, 0:TK]
+
+        def ecol(n):
+            j = T.rank_of(group[order[n]])
+            return ex[0:TK, j:j + 1]
+
         g.tensor.matmul(T.st[0:TK, 0:16], xh, T.rts[:], True, True).then_inc(s["st"], 1)
         g.tensor.transpose(T.xt[0:TK, 0:128], xh, T.ident[:]).then_inc(s["xt"], 1)
         g.vector.wait_ge(s["st"], 1)
@@ -92,49 +104,55 @@ def rank_program(g, core, T, topo):
         g.scalar.wait_ge(s["nm"], 1)
         g.scalar.activation(ex[0:TK, :], T.st[0:TK, 0:16], ActivationFunctionType.Exp, bias=nm, scale=1.0,
                             accum_out=su).then_inc(s["ex"], 1)
-        g.vector.wait_ge(s["xt"], 1)
-        g.vector.tensor_copy(xts[0:TK, :], T.xt[0:TK, 0:128]).then_inc(s["xts"], 1)
+        g.scalar.wait_ge(s["ex"], 1)
+        for n in range(NS):
+            g.scalar.activation(dg[0:TK, n * TK:(n + 1) * TK], eye, ActivationFunctionType.Copy,
+                                scale=ecol(n)).then_inc(s["d%d" % (n // EP)], 1)
         g.vector.wait_ge(s["ex"], 1)
         g.vector.reciprocal(ri, su).then_inc(s["ri"], 1)
         g.vector.wait_ge(s["ri"], 1)
-        for i, q in enumerate(group):
-            j = T.rank_of(q)
-            g.vector.tensor_scalar(dg[0:TK, i * TK:(i + 1) * TK], T.ident[0:TK, 0:TK], ex[0:TK, j:j + 1], ri,
-                                   AluOpType.mult, AluOpType.mult).then_inc(s["da"] if i < H else s["db"], 1)
+        g.vector.wait_ge(s["xt"], 1)
+        g.vector.tensor_scalar(xts[0:TK, :], T.xt[0:TK, 0:128], ri, None, AluOpType.mult).then_inc(s["xts"], 1)
+        for n in range(NS, NG):
+            g.vector.tensor_scalar(dg[0:TK, n * TK:(n + 1) * TK], eye, ecol(n), None,
+                                   AluOpType.mult).then_inc(s["d%d" % (n // EP)], 1)
         g.tensor.wait_ge(s["xts"], 1)
-        if not first:
-            g.tensor.wait_ge(S.ca_o, 1)
-            g.tensor.wait_ge(S.cb_o, 1)
-        g.tensor.wait_ge(s["da"], H)
-        g.tensor.matmul(T.pga[:, 0:H * TK], xts[0:TK, :], dg[0:TK, 0:H * TK], True, True).then_inc(s["pa"], 1)
-        g.tensor.wait_ge(s["db"], NG - H)
-        g.tensor.matmul(T.pgb[:, 0:H * TK], xts[0:TK, :], dg[0:TK, H * TK:NG * TK], True, True).then_inc(s["pb"], 1)
-        g.vector.wait_ge(s["pa"], 1)
-        g.vector.tensor_copy(xg[:, 0:H * TK], T.pga[:, 0:H * TK]).then_inc(s["ca"], 1)
-        g.scalar.wait_ge(s["pb"], 1)
-        g.scalar.activation(xg[:, H * TK:NG * TK], T.pgb[:, 0:H * TK], ActivationFunctionType.Copy).then_inc(s["cb"], 1)
+        W = EP * TK
+        for q in range(NP):
+            pg = T["pg%d" % q]
+            if not first:
+                g.tensor.wait_ge(S["c%d_o" % q], 1)
+            g.tensor.wait_ge(s["d%d" % q], EP)
+            g.tensor.matmul(pg[:, 0:W], xts[0:TK, :], dg[0:TK, q * W:(q + 1) * W], True, True).then_inc(s["p%d" % q], 1)
+            if q % 2 == 0:
+                g.vector.wait_ge(s["p%d" % q], 1)
+                g.vector.tensor_copy(xg[:, q * W:(q + 1) * W], pg[:, 0:W]).then_inc(s["c%d" % q], 1)
+            else:
+                g.scalar.wait_ge(s["p%d" % q], 1)
+                g.scalar.activation(xg[:, q * W:(q + 1) * W], pg[:, 0:W],
+                                    ActivationFunctionType.Copy).then_inc(s["c%d" % q], 1)
 
     g.tensor.wait_ge(S.ldx, 16)
     g.tensor.wait_ge(S.ldrt, 16)
     g.tensor.wait_ge(S.idn, 1)
     g.vector.wait_ge(S.idn, 1)
+    g.scalar.wait_ge(S.idn, 1)
     half("o", T.xs[:, 0:TK], True)
     g.tensor.wait_ge(S.xarr, _engines(pmask))
     half("p", T.xs[:, TK:2 * TK], False)
 
-    g.tensor.wait_ge(S.ca_p, 1)
-    g.tensor.wait_ge(S.cb_p, 1)
-    order = [me] + [(me - k) % NG for k in range(1, NG)]
     for n, i in enumerate(order):
+        if n % EP == 0:
+            g.tensor.wait_ge(S["c%d_p" % (n // EP)], 1)
         if i == me:
             g.tensor.wait_ge(S.ldw, 16)
         else:
             g.tensor.wait_ge(S["w%d" % i], _engines(wmask))
-        a = g.tensor.matmul(T.acc_p[:, 0:TK], slot(i), T.xg_p[:, i * TK:(i + 1) * TK], n == 0, n == NG - 1)
-        b = g.tensor.matmul(T.acc_o[:, 0:TK], slot(i), T.xg_o[:, i * TK:(i + 1) * TK], n == 0, n == NG - 1)
-        if n == NG - 1:
-            a.then_inc(S.accp, 1)
-            b.then_inc(S.acco, 1)
+        a = g.tensor.matmul(T.acc_p[:, 0:TK], slot(i), T.xg_p[:, n * TK:(n + 1) * TK], n == 0, n == NG - 1)
+    a.then_inc(S.accp, 1)
+    for n, i in enumerate(order):
+        b = g.tensor.matmul(T.acc_o[:, 0:TK], slot(i), T.xg_o[:, n * TK:(n + 1) * TK], n == 0, n == NG - 1)
+    b.then_inc(S.acco, 1)
 
     g.vector.wait_ge(S.accp, 1)
     g.vector.tensor_copy(T.yp[:], T.acc_p[:, 0:TK]).then_inc(S.ypr, 1)

from concourse.bass import DstId, RemoteDMATransfer
from concourse.mybir import AluOpType, AxisListType, ActivationFunctionType

NG = 8
TK = 64
DM = 128
NP = 4
EP = NG // NP
NS = 6

SCRATCH = {
    "xs": ("sbuf", [128, 2 * TK], "bfloat16"),
    "rts": ("sbuf", [128, 16], "bfloat16"),
    "wall": ("sbuf", [128, NG * DM], "bfloat16"),
    "ident": ("sbuf", [128, 128], "bfloat16"),
    "sm_o": ("sbuf", [128, 4], "float32"),
    "sm_p": ("sbuf", [128, 4], "float32"),
    "ex_o": ("sbuf", [128, 16], "float32"),
    "ex_p": ("sbuf", [128, 16], "float32"),
    "xts_o": ("sbuf", [128, 128], "bfloat16"),
    "xts_p": ("sbuf", [128, 128], "bfloat16"),
    "dg_o": ("sbuf", [128, NG * TK], "bfloat16"),
    "dg_p": ("sbuf", [128, NG * TK], "bfloat16"),
    "xg_o": ("sbuf", [128, NG * TK], "bfloat16"),
    "xg_p": ("sbuf", [128, NG * TK], "bfloat16"),
    "yp": ("sbuf", [128, TK], "bfloat16"),
    "yr": ("sbuf", [128, TK], "bfloat16"),
    "ysb": ("sbuf", [128, TK], "bfloat16"),
    "st": ("psum", [128, 512], "float32"),
    "xt": ("psum", [128, 1024], "bfloat16"),
    "pg0": ("psum", [128, 512], "float32"),
    "pg1": ("psum", [128, 512], "float32"),
    "pg2": ("psum", [128, 512], "float32"),
    "pg3": ("psum", [128, 512], "float32"),
    "acc_p": ("psum", [128, 512], "float32"),
    "acc_o": ("psum", [128, 512], "float32"),
}
_STAGES = (["st", "xt", "nm", "ex", "ri", "xts"] + ["d%d" % q for q in range(NP)] + ["p%d" % q for q in range(NP)]
           + ["c%d" % q for q in range(NP)])
SEMAPHORES = (["ldx", "ldw", "ldrt", "ones", "idn", "xarr", "sent", "accp", "acco", "ypr", "yarr", "ysum", "stored"]
              + ["w%d" % i for i in range(NG)]
              + [s + "_" + h for h in ("o", "p") for s in _STAGES])


def _engines(mask):
    return bin(mask).count("1")


def rank_program(g, core, T, topo):
    if T.rank_of(core) is None:
        return
    S = T.sem
    cores = list(T.cores)
    group = [q for q in cores if q == core or topo.same_plane(core, q)]
    me = group.index(core)
    partner = [q for q in cores if topo.rack(topo.host(q)) != topo.rack(topo.host(core))
               and topo.may_write(core, q) and topo.chip(q) == topo.chip(core)][0]
    peers = [group[(me + k) % NG] for k in range(1, NG)]
    order = [me] + [(me - k) % NG for k in range(1, NG)]

    def slot(i):
        return T.wall[:, i * DM:(i + 1) * DM]

    g.sync.dma_start(T.xs[:, 0:TK], T.x[:]).then_inc(S.ldx, 16)
    g.scalar.dma_start(slot(me), T.w[:]).then_inc(S.ldw, 16)
    g.sync.dma_start(T.rts[:], T.rt[:]).then_inc(S.ldrt, 16)

    g.vector.memset(T.ident[:], 1.0).then_inc(S.ones, 1)
    g.wait_ge(S.ones, 1)
    g.affine_select(T.ident[:], T.ident[:], [[-1, 128]], AluOpType.is_equal, 0.0, 0, 1).then_inc(S.idn, 1)

    prid, ppid = topo.addr(partner, core)
    pmask = topo.mask(core, partner)
    g.wait_ge(S.ldx, 16)
    g.remote_dma(out_ap=T.xs[:, TK:2 * TK], in_ap=T.xs[:, 0:TK], remote_sem=S.xarr, local_sem=S.sent,
                 pid=ppid, routing_id=prid, dma_engine_mask=pmask)

    wmask = pmask
    for q in peers:
        wmask &= topo.mask(core, q)
    ids = []
    for q in peers:
        rid, pid = topo.addr(q, core)
        ids.append(DstId(rid=rid, pnc=pid))
    g.wait_ge(S.ldw, 16)
    g.remote_dma_fused([RemoteDMATransfer(dst_ids=ids, dma_engine_mask=wmask, remote_sem=S["w%d" % me],
                                          srcs=[slot(me)], dsts=[slot(me) for _ in peers], alu_op=0)],
                       local_sem=S.sent)

    def half(h, xh, first):
        sm, ex, xts, dg, xg = T["sm_" + h], T["ex_" + h], T["xts_" + h], T["dg_" + h], T["xg_" + h]
        s = {n: S[n + "_" + h] for n in _STAGES}
        nm, su, ri = sm[0:TK, 0:1], sm[0:TK, 1:2], sm[0:TK, 2:3]
        eye = T.ident[0:TK, 0:TK]

        def ecol(n):
            j = T.rank_of(group[order[n]])
            return ex[0:TK, j:j + 1]

        g.tensor.matmul(T.st[0:TK, 0:16], xh, T.rts[:], True, True).then_inc(s["st"], 1)
        g.tensor.transpose(T.xt[0:TK, 0:128], xh, T.ident[:]).then_inc(s["xt"], 1)
        g.vector.wait_ge(s["st"], 1)
        g.vector.tensor_reduce(nm, T.st[0:TK, 0:16], AxisListType.X, AluOpType.max, negate=True).then_inc(s["nm"], 1)
        g.scalar.wait_ge(s["nm"], 1)
        g.scalar.activation(ex[0:TK, :], T.st[0:TK, 0:16], ActivationFunctionType.Exp, bias=nm, scale=1.0,
                            accum_out=su).then_inc(s["ex"], 1)
        g.scalar.wait_ge(s["ex"], 1)
        for n in range(NS):
            g.scalar.activation(dg[0:TK, n * TK:(n + 1) * TK], eye, ActivationFunctionType.Copy,
                                scale=ecol(n)).then_inc(s["d%d" % (n // EP)], 1)
        g.vector.wait_ge(s["ex"], 1)
        g.vector.reciprocal(ri, su).then_inc(s["ri"], 1)
        g.vector.wait_ge(s["ri"], 1)
        g.vector.wait_ge(s["xt"], 1)
        g.vector.tensor_scalar(xts[0:TK, :], T.xt[0:TK, 0:128], ri, None, AluOpType.mult).then_inc(s["xts"], 1)
        for n in range(NS, NG):
            g.vector.tensor_scalar(dg[0:TK, n * TK:(n + 1) * TK], eye, ecol(n), None,
                                   AluOpType.mult).then_inc(s["d%d" % (n // EP)], 1)
        g.tensor.wait_ge(s["xts"], 1)
        W = EP * TK
        for q in range(NP):
            pg = T["pg%d" % q]
            if not first:
                g.tensor.wait_ge(S["c%d_o" % q], 1)
            g.tensor.wait_ge(s["d%d" % q], EP)
            g.tensor.matmul(pg[:, 0:W], xts[0:TK, :], dg[0:TK, q * W:(q + 1) * W], True, True).then_inc(s["p%d" % q], 1)
            if q % 2 == 0:
                g.vector.wait_ge(s["p%d" % q], 1)
                g.vector.tensor_copy(xg[:, q * W:(q + 1) * W], pg[:, 0:W]).then_inc(s["c%d" % q], 1)
            else:
                g.scalar.wait_ge(s["p%d" % q], 1)
                g.scalar.activation(xg[:, q * W:(q + 1) * W], pg[:, 0:W],
                                    ActivationFunctionType.Copy).then_inc(s["c%d" % q], 1)

    g.tensor.wait_ge(S.ldx, 16)
    g.tensor.wait_ge(S.ldrt, 16)
    g.tensor.wait_ge(S.idn, 1)
    g.vector.wait_ge(S.idn, 1)
    g.scalar.wait_ge(S.idn, 1)
    half("o", T.xs[:, 0:TK], True)
    g.tensor.wait_ge(S.xarr, _engines(pmask))
    half("p", T.xs[:, TK:2 * TK], False)

    for n, i in enumerate(order):
        if n % EP == 0:
            g.tensor.wait_ge(S["c%d_p" % (n // EP)], 1)
        if i == me:
            g.tensor.wait_ge(S.ldw, 16)
        else:
            g.tensor.wait_ge(S["w%d" % i], _engines(wmask))
        a = g.tensor.matmul(T.acc_p[:, 0:TK], slot(i), T.xg_p[:, n * TK:(n + 1) * TK], n == 0, n == NG - 1)
    a.then_inc(S.accp, 1)
    for n, i in enumerate(order):
        b = g.tensor.matmul(T.acc_o[:, 0:TK], slot(i), T.xg_o[:, n * TK:(n + 1) * TK], n == 0, n == NG - 1)
    b.then_inc(S.acco, 1)

    g.vector.wait_ge(S.accp, 1)
    g.vector.tensor_copy(T.yp[:], T.acc_p[:, 0:TK]).then_inc(S.ypr, 1)
    g.wait_ge(S.ypr, 1)
    g.remote_dma(out_ap=T.yr[:], in_ap=T.yp[:], remote_sem=S.yarr, local_sem=S.sent,
                 pid=ppid, routing_id=prid, dma_engine_mask=pmask)

    g.vector.wait_ge(S.acco, 1)
    g.vector.wait_ge(S.yarr, _engines(pmask))
    g.vector.tensor_tensor(T.ysb[:], T.acc_o[:, 0:TK], T.yr[:], AluOpType.add).then_inc(S.ysum, 1)
    g.sync.wait_ge(S.ysum, 1)
    g.sync.dma_start(T.y[:], T.ysb[:]).then_inc(S.stored, 16)
    g.sync.wait_ge(S.stored, 16)
    g.wait_ge(S.sent, 2 * _engines(pmask) + _engines(wmask))
